import numpy as np
CORES = [6,22,38,54,70,86,102,118]
N = 8
def setup_inputs(rng):
    return {"x": rng.standard_normal((N, 128, 256), dtype=np.float32)}
def reference(x):
    b = 256 // N
    blocks = x.reshape(N, 128, N, b)
    return {"y": np.ascontiguousarray(blocks.transpose(2, 1, 0, 3)).reshape(N, 128, 256)}

@@ -1,0 +1,42 @@
+from concourse.bass import DstId, RemoteDMATransfer
+
+N = 8
+B = 256 // N
+
+SCRATCH = {
+    "send": ("sbuf", [128, 256], "float32"),
+    "land": ("sbuf", [128, 256], "float32"),
+}
+SEMAPHORES = ["loaded", "own", "arrived", "read", "stored"]
+
+
+def rank_program(g, core, T, topo):
+    r = T.rank_of(core)
+    if r is None:
+        return
+
+    def blk(j):
+        return slice(j * B, (j + 1) * B)
+
+    g.sync.dma_start(T.send[:], T.x[:]).then_inc(T.sem.loaded, 16)
+    g.scalar.dma_start(T.land[:, blk(r)], T.x[:, blk(r)]).then_inc(T.sem.own, 16)
+
+    transfers = []
+    for k in range(N - 1):
+        j = (r + 1 + k) % N
+        rid, pid, _se = topo.addr(T.cores[j])
+        transfers.append(RemoteDMATransfer(
+            dst_ids=[DstId(rid=rid, pnc=pid)],
+            dma_engine_mask=1 << k,
+            remote_sem=T.sem.arrived,
+            src=T.send[:, blk(j)],
+            dst=T.land[:, blk(r)],
+        ))
+    g.wait_ge(T.sem.loaded, 16)
+    g.remote_dma_fused(transfers, local_sem=T.sem.read)
+
+    g.sync.wait_ge(T.sem.own, 16)
+    g.sync.wait_ge(T.sem.arrived, N - 1)
+    g.sync.dma_start(T.y[:], T.land[:]).then_inc(T.sem.stored, 16)
+    g.sync.wait_ge(T.sem.stored, 16)
+    g.wait_ge(T.sem.read, N - 1)

@@ -22,8 +22,7 @@ def rank_program(g, core, T, topo):
     g.scalar.dma_start(T.land[:, blk(r)], T.x[:, blk(r)]).then_inc(T.sem.own, 16)
 
     transfers = []
-    for k in range(N - 1):
-        j = (r + 1 + k) % N
+    for k, j in enumerate(j for j in range(N) if j != r):
         rid, pid, _se = topo.addr(T.cores[j])
         transfers.append(RemoteDMATransfer(
             dst_ids=[DstId(rid=rid, pnc=pid)],

from concourse.bass import DstId, RemoteDMATransfer

N = 8
B = 256 // N

SCRATCH = {
    "send": ("sbuf", [128, 256], "float32"),
    "land": ("sbuf", [128, 256], "float32"),
}
SEMAPHORES = ["loaded", "own", "arrived", "read", "stored"]


def rank_program(g, core, T, topo):
    r = T.rank_of(core)
    if r is None:
        return

    def blk(j):
        return slice(j * B, (j + 1) * B)

    g.sync.dma_start(T.send[:], T.x[:]).then_inc(T.sem.loaded, 16)
    g.scalar.dma_start(T.land[:, blk(r)], T.x[:, blk(r)]).then_inc(T.sem.own, 16)

    transfers = []
    for k, j in enumerate(j for j in range(N) if j != r):
        rid, pid, _se = topo.addr(T.cores[j])
        transfers.append(RemoteDMATransfer(
            dst_ids=[DstId(rid=rid, pnc=pid)],
            dma_engine_mask=1 << k,
            remote_sem=T.sem.arrived,
            src=T.send[:, blk(j)],
            dst=T.land[:, blk(r)],
        ))
    g.wait_ge(T.sem.loaded, 16)
    g.remote_dma_fused(transfers, local_sem=T.sem.read)

    g.sync.wait_ge(T.sem.own, 16)
    g.sync.wait_ge(T.sem.arrived, N - 1)
    g.sync.dma_start(T.y[:], T.land[:]).then_inc(T.sem.stored, 16)
    g.sync.wait_ge(T.sem.stored, 16)
    g.wait_ge(T.sem.read, N - 1)
